import numpy as np
import ml_dtypes


def mxq(x, axis, fmt="e4m3"):
    dtype, down = {"e4m3": (ml_dtypes.float8_e4m3fn, 7), "e5m2": (ml_dtypes.float8_e5m2, 14)}[fmt]
    v = np.moveaxis(np.asarray(x, np.float32).astype(ml_dtypes.bfloat16).astype(np.float64), axis, -1)
    blocks = v.reshape(v.shape[:-1] + (-1, 32))
    amax = np.abs(blocks).max(-1, keepdims=True)
    byte = np.maximum(np.where(amax > 0, np.frexp(amax)[1] - 1 + 127, 0) - down, 1)
    scale = np.exp2(byte - 127.0)
    codes = (blocks / scale).astype(np.float32).astype(dtype).astype(np.float64)
    return np.moveaxis((codes * scale).reshape(v.shape), -1, axis)


WIDE = False


def mx_kscale(k):
    if not WIDE:
        return np.ones(k)
    levels = np.array([10, -10, 5, -5, 0])
    if k % 512:
        return np.exp2(np.random.permutation(np.resize(levels, k // 32))).repeat(32)
    a = np.empty((k // 512, 16))
    for p in range(k // 512):
        a[p, :8] = np.random.permutation(np.resize(levels, 8))
        for g in range(8):
            far = levels[np.abs(levels - a[p, g]) >= 10]
            a[p, g + 8] = far[np.random.randint(len(far))]
    return np.exp2(a.ravel()).repeat(32)


def f64(x):
    return np.asarray(x).astype(np.float64)


def striped(idx):
    return np.tile(np.asarray(idx).reshape(-1, 16).T, (8, 1)).astype(np.uint16)


def unstriped(offs):
    return offs[:16].T.reshape(-1).astype(np.int64)


E2M1 = np.array([0.0, 0.5, 1.0, 1.5, 2.0, 3.0, 4.0, 6.0, -0.0, -0.5, -1.0, -1.5, -2.0, -3.0, -4.0, -6.0])


def pack_weight(w, fmt):
    k, n = w.shape
    w = f64(np.asarray(w, np.float32).astype(ml_dtypes.bfloat16)).reshape(k // 32, 32, n)
    amax = np.abs(w).max(1)
    if fmt == "e4m3":
        byte = np.frexp(amax)[1] - 1 + 127 - 7
    else:
        mant, ex = np.frexp(amax / 6.0)
        byte = np.where(mant > 0.5, ex, ex - 1) + 127
    byte = np.clip(np.where(amax > 0, byte, 1), 1, 254)
    scaled = (w * np.exp2(127.0 - byte)[:, None, :]).reshape(k, n).astype(np.float32)
    by_word = np.ascontiguousarray(scaled.reshape(k // 512, 128, 4, n).transpose(0, 1, 3, 2))
    if fmt == "e4m3":
        words = by_word.astype(ml_dtypes.float8_e4m3fn).view(np.uint8)
    else:
        c = by_word.astype(ml_dtypes.float4_e2m1fn).view(np.uint8) & 0xF
        words = (c[..., 0::2] | (c[..., 1::2] << 4)).reshape(k // 512, 128, 2 * n)
    return np.ascontiguousarray(words), np.ascontiguousarray(byte.astype(np.uint8).reshape(k // 512, 16, n))


def unpack_weight(words, scales, fmt):
    g, _, n = scales.shape
    words = np.ascontiguousarray(words).reshape(g, 128, n, -1)
    if fmt == "e4m3":
        vals = words.view(ml_dtypes.float8_e4m3fn).astype(np.float64)
    else:
        nib = np.empty((g, 128, n, 4), np.uint8)
        nib[..., 0::2] = words & 0xF
        nib[..., 1::2] = words >> 4
        vals = E2M1[nib]
    vals = vals * np.repeat(np.exp2(scales.astype(np.float64) - 127.0), 8, axis=1)[..., None]
    return vals.transpose(0, 1, 3, 2).reshape(g * 512, n)


def softplus(v):
    return np.log(1.0 + np.exp(v))


def sigmoid(v):
    return 1.0 / (1.0 + np.exp(-v))


K, R, F, T, J, M = 512, 128, 512, 2048, 512, 256


def setup_inputs():
    n = np.random.standard_normal
    idx = np.random.permutation(T)[:J]
    idx2 = np.random.permutation(J)[:M]
    idx3 = np.random.permutation(J)[:M]
    idx4 = np.random.permutation(J)[:M]
    fk = mx_kscale(K)
    ff = mx_kscale(F)
    tabp = pack_weight(n((K, T)) / fk[:, None], "e4m3")
    return {
        "tab_words": tabp[0],
        "tab_scales": tabp[1],
        "w1": (n((K, R)) * 1 / np.sqrt(K) * fk[:, None]).astype(np.float32),
        "bias": (np.random.uniform(-0.5, 0.5, (R, 1))).astype(np.float32),
        "wo": (n((F, R)) * 1 / np.sqrt(F) * ff[:, None]).astype(np.float32),
        "dy": (n((F, M)) / ff[:, None]).astype(np.float32),
        "old": (0.5 * n((R, J))).astype(np.float32),
        "offs": striped(idx),
        "offs2": striped(idx2),
        "offs3": striped(idx3),
        "offs4": striped(idx4),
    }


def reference(tab_words, tab_scales, w1, bias, wo, dy, old, offs, offs2, offs3, offs4):
    idx = unstriped(offs)
    idx2 = unstriped(offs2)
    idx3 = unstriped(offs3)
    idx4 = unstriped(offs4)
    tabu = unpack_weight(tab_words, tab_scales, "e4m3")
    w1q = mxq(f64(w1), 0, "e4m3")
    tabidxg = tabu[:, idx]
    a = w1q.T @ tabidxg
    h1 = softplus(a + f64(bias))
    s = h1[:, idx2] * h1[:, idx3] * h1[:, idx4]
    woq = mxq(f64(wo), 0, "e4m3")
    dyq = mxq(f64(dy), 0, "e4m3")
    c0 = woq.T @ dyq
    ds = c0 / (s + 1.0)
    e1 = ds * h1[:, idx4] * h1[:, idx3]
    s1 = np.zeros((R, J))
    s1[:, idx2] = e1
    e2 = ds * h1[:, idx4] * h1[:, idx2]
    s2 = np.zeros((R, J))
    s2[:, idx3] = e2
    e3 = ds * h1[:, idx2] * h1[:, idx3]
    s3 = np.zeros((R, J))
    s3[:, idx4] = e3
    dh1 = s1 + s2 + s3
    da = dh1 * sigmoid(a + f64(bias))
    y = da + f64(old)
    return y

@@ -1,0 +1,201 @@
+from contextlib import ExitStack
+
+import concourse.mybir as mybir
+from concourse.masks import make_identity
+
+K, R, F, T, J, M = 512, 128, 512, 2048, 512, 256
+FLOPS = 2 * K * R * J + 2 * F * R * M
+
+F32 = mybir.dt.float32
+BF16 = mybir.dt.bfloat16
+I32 = mybir.dt.int32
+U32 = mybir.dt.uint32
+U16 = mybir.dt.uint16
+U8 = mybir.dt.uint8
+FP8X4 = mybir.dt.float8_e4m3fn_x4
+ALU = mybir.AluOpType
+ACT = mybir.ActivationFunctionType
+
+P = 128
+PACK = 4
+HALF = J // 2
+LN_FLOOR = 2.0 ** -60
+
+
+def tile_attend_ctriples_kernel(tc, tab_words, tab_scales, w1, bias, wo, dy, old, offs, offs2, offs3, offs4, out):
+    nc = tc.nc
+    halves = [slice(0, HALF), slice(HALF, J)]
+
+    with ExitStack() as ctx:
+        sb = ctx.enter_context(tc.tile_pool(name="sb", bufs=1))
+        psum = ctx.enter_context(tc.psum_pool(name="psum", bufs=1))
+
+        def load_list(name, src):
+            t = sb.tile(list(src.shape), U16, name=name)
+            nc.sync.dma_start(t[:], src)
+            return t
+
+        def load_rows(name, src):
+            t = sb.tile([P, PACK, src.shape[1]], F32, name=name)
+            nc.sync.dma_start(t[:], src.rearrange("(p j) w -> p j w", j=PACK))
+            return t
+
+        def interleave(t, raw):
+            nc.vector.tensor_copy(
+                out=t.rearrange("p (c i) j -> p c j i", i=4),
+                in_=raw[:].rearrange("p j (c i) -> p c j i", i=4),
+            )
+
+        def quantise(name, grouped):
+            width = grouped.shape[1]
+            codes = sb.tile([P, width], U32, name=name + "_codes", align_bytes=64)
+            scales = sb.tile([P, width], U8, name=name + "_scales", align_bytes=64)
+            nc.vector.quantize_mx(
+                out=codes[:].bitcast(FP8X4), scales=scales[:], in_=grouped.rearrange("p w j -> p (w j)")
+            )
+            return codes, scales
+
+        tab_s = sb.tile([P, T], U8, name="tab_s", tag="tab_s", align_bytes=64)
+        nc.gpsimd.memset(tab_s[:].bitcast(I32), 0)
+        idx = load_list("idx", offs)
+        w1_raw = load_rows("w1_raw", w1)
+        for q in range(4):
+            nc.sync.dma_start(tab_s[q:P:32, :].bitcast(I32), tab_scales[0, q:16:4, :].bitcast(I32))
+        tab_w = sb.tile([P, T], I32, name="tab_w", tag="tab_w", align_bytes=64)
+        nc.sync.dma_start(tab_w[:], tab_words[0].rearrange("p n t -> p (n t)").bitcast(I32))
+        b = sb.tile([P, 1], F32, name="b")
+        nc.sync.dma_start(b[:], bias)
+        wo_raw = load_rows("wo_raw", wo)
+        dy_raw = load_rows("dy_raw", dy)
+        idx2 = load_list("idx2", offs2)
+        idx3 = load_list("idx3", offs3)
+        idx4 = load_list("idx4", offs4)
+        old_sb = sb.tile([P, J], F32, name="old_sb")
+        nc.sync.dma_start(old_sb[:], old)
+
+        s1 = sb.tile([P, J], F32, name="s1")
+        s2 = sb.tile([P, J], F32, name="s2")
+        s3 = sb.tile([P, J], F32, name="s3")
+        for window in (s1, s2, s3):
+            nc.gpsimd.memset(window[:], 0.0)
+
+        ident = sb.tile([P, P], F32, name="ident")
+        make_identity(nc, ident[:])
+
+        warm_sig = sb.tile([P, 1], F32, name="warm_sig")
+        nc.scalar.activation(warm_sig[:], s1[:, 0:1], ACT.Sigmoid)
+        neg_b = sb.tile([P, 1], F32, name="neg_b")
+        nc.scalar.activation(neg_b[:], b[:], ACT.Copy, scale=-1.0)
+
+        w1_bf = sb.tile([P, R, PACK], BF16, name="w1_bf", tag="w1_bf", align_bytes=64)
+        interleave(w1_bf[:], w1_raw)
+        w1_c, w1_s = quantise("w1", w1_bf[:])
+        col_s = sb.tile([P, J], U8, name="col_s", tag="w1_bf", align_bytes=64)
+        nc.vector.tensor_copy(col_s[:], tab_s[:].indirect(idx[:]))
+        a = []
+        for h, cols in enumerate(halves):
+            col_w = sb.tile([P, HALF], U32, name=f"col_w{h}", tag=("tab_s", "col_w1")[h], align_bytes=64)
+            nc.vector.tensor_copy(
+                col_w[:], tab_w[:].bitcast(U32).indirect(idx[:, h * HALF // 16 : (h + 1) * HALF // 16])
+            )
+            acc = psum.tile([P, HALF], F32, name=f"a{h}", tag=f"half{h}")
+            nc.tensor.matmul_mx(
+                out=acc[:], lhsT=w1_c[:].bitcast(FP8X4), lhsT_scale=w1_s[:],
+                rhs=col_w[:].bitcast(FP8X4), rhs_scale=col_s[:, cols], start=True, stop=True,
+            )
+            a.append(acc)
+
+        sig_neg = sb.tile([P, J], F32, name="sig_neg")
+        z = sb.tile([P, J], F32, name="z")
+        for h, cols in enumerate(halves):
+            nc.scalar.activation(sig_neg[:, cols], a[h][:], ACT.Sigmoid, bias=neg_b[:], scale=-1.0)
+        for h, cols in enumerate(halves):
+            nc.vector.tensor_scalar(z[:, cols], a[h][:], b[:], None, ALU.add)
+
+        back_bf = sb.tile([P, R + M, PACK], BF16, name="back_bf", tag="tab_w", align_bytes=64)
+        interleave(back_bf[:, :R, :], wo_raw)
+        interleave(back_bf[:, R:, :], dy_raw)
+        wo_c, wo_s = quantise("wo", back_bf[:, :R, :])
+        dy_c, dy_s = quantise("dy", back_bf[:, R:, :])
+        c0 = psum.tile([P, M], F32, name="c0")
+        nc.tensor.matmul_mx(
+            out=c0[:], lhsT=wo_c[:].bitcast(FP8X4), lhsT_scale=wo_s[:],
+            rhs=dy_c[:].bitcast(FP8X4), rhs_scale=dy_s[:], start=True, stop=True,
+        )
+
+        ln_sig = sb.tile([P, J], F32, name="ln_sig")
+        h1 = sb.tile([P, J], F32, name="h1")
+        for cols in halves:
+            nc.scalar.activation(ln_sig[:, cols], sig_neg[:, cols], ACT.Ln, bias=LN_FLOOR)
+            nc.vector.scalar_tensor_tensor(h1[:, cols], ln_sig[:, cols], -1.0, z[:, cols], ALU.mult, ALU.max)
+        warm_rs = sb.tile([P, 1], F32, name="warm_rs")
+        nc.scalar.activation(warm_rs[:], ln_sig[:, J - 1 : J], ACT.Abs_reciprocal_sqrt, bias=1.0, scale=-1.0)
+
+        g2 = sb.tile([P, M], F32, name="g2")
+        g3 = sb.tile([P, M], F32, name="g3")
+        g4 = sb.tile([P, M], F32, name="g4")
+        g23 = sb.tile([P, M], F32, name="g23")
+        s = sb.tile([P, M], F32, name="s")
+        parts = [slice(0, M // 2), slice(M // 2, M)]
+        lists = [slice(0, M // 32), slice(M // 32, M // 16)]
+        c23 = sb.tile([P, M], F32, name="c23")
+        c4 = sb.tile([P, M], F32, name="c4")
+        ds4 = sb.tile([P, M], F32, name="ds4")
+        root = sb.tile([P, M], F32, name="root", tag="late")
+        inv = sb.tile([P, M], F32, name="inv")
+
+        def look_up(g, lst, i):
+            nc.vector.tensor_copy(g[:, parts[i]], h1[:].indirect(lst[:, lists[i]]))
+
+        def times(product, x, y, i):
+            nc.vector.tensor_tensor(product[:, parts[i]], x[:, parts[i]], y[:, parts[i]], ALU.mult)
+
+        def invert(i):
+            nc.scalar.activation(root[:, parts[i]], s[:, parts[i]], ACT.Abs_reciprocal_sqrt, bias=1.0)
+            nc.scalar.activation(inv[:, parts[i]], root[:, parts[i]], ACT.Square)
+
+        def place_e3(i):
+            nc.vector.tensor_tensor(s3[:].indirect(idx4[:, lists[i]]), c23[:, parts[i]], inv[:, parts[i]], ALU.mult)
+
+        nc.vector.tensor_copy(g2[:], h1[:].indirect(idx2[:]))
+        look_up(g3, idx3, 0)
+        look_up(g4, idx4, 0)
+        times(g23, g2, g3, 0)
+        look_up(g3, idx3, 1)
+        times(s, g23, g4, 0)
+        invert(0)
+        look_up(g4, idx4, 1)
+        times(g23, g2, g3, 1)
+        times(c23, c0, g23, 0)
+        times(s, g23, g4, 1)
+        invert(1)
+        nc.vector.tensor_tensor(c4[:], c0[:], g4[:], ALU.mult)
+        times(c23, c0, g23, 1)
+        place_e3(0)
+        nc.vector.tensor_tensor(ds4[:], c4[:], inv[:], ALU.mult)
+        place_e3(1)
+        nc.vector.tensor_tensor(s1[:].indirect(idx2[:]), ds4[:], g3[:], ALU.mult)
+        nc.vector.tensor_tensor(s2[:].indirect(idx3[:]), ds4[:], g2[:], ALU.mult)
+        sig = sb.tile([P, J], F32, name="sig", tag="late")
+        nc.scalar.activation(sig[:], z[:], ACT.Sigmoid)
+
+        blocks = [slice(i * P, (i + 1) * P) for i in range(J // P)]
+        turned = [psum.tile([P, P], F32, name=f"turned{i}") for i in range(len(blocks))]
+        for i, cols in enumerate(blocks):
+            nc.tensor.matmul(turned[i][:], s3[:, cols], ident[:], start=True, stop=False, is_transpose=True)
+        turned_sb = sb.tile([P, J], F32, name="turned_sb")
+        for i, cols in enumerate(blocks):
+            nc.tensor.matmul(turned[i][:], s1[:, cols], ident[:], start=False, stop=True, is_transpose=True)
+            nc.scalar.copy(turned_sb[:, cols], turned[i][:])
+        s13 = [psum.tile([P, HALF], F32, name=f"s13_{h}", tag=f"half{h}") for h in range(2)]
+        for i, cols in enumerate(blocks):
+            nc.tensor.transpose(s13[i // 2][:, blocks[i % 2]], turned_sb[:, cols], ident[:])
+
+        y = [sb.tile([P, HALF], F32, name=f"y{h}") for h in range(2)]
+        for h, cols in enumerate(halves):
+            nc.vector.tensor_tensor(y[h][:], s13[h][:], s2[:, cols], ALU.add)
+        for h, cols in enumerate(halves):
+            nc.vector.tensor_tensor(y[h][:], y[h][:], sig[:, cols], ALU.mult)
+        for h, cols in enumerate(halves):
+            nc.vector.tensor_tensor(y[h][:], y[h][:], old_sb[:, cols], ALU.add)
+            nc.sync.dma_start(out[:, cols], y[h][:])

@@ -25,6 +25,7 @@ LN_FLOOR = 2.0 ** -60
 def tile_attend_ctriples_kernel(tc, tab_words, tab_scales, w1, bias, wo, dy, old, offs, offs2, offs3, offs4, out):
     nc = tc.nc
     halves = [slice(0, HALF), slice(HALF, J)]
+    blocks = [slice(i * P, (i + 1) * P) for i in range(J // P)]
 
     with ExitStack() as ctx:
         sb = ctx.enter_context(tc.tile_pool(name="sb", bufs=1))
@@ -56,9 +57,9 @@ def tile_attend_ctriples_kernel(tc, tab_words, tab_scales, w1, bias, wo, dy, old
             return codes, scales
 
         tab_s = sb.tile([P, T], U8, name="tab_s", tag="tab_s", align_bytes=64)
-        nc.gpsimd.memset(tab_s[:].bitcast(I32), 0)
-        idx = load_list("idx", offs)
+        nc.vector.memset(tab_s[:].bitcast(I32), 0)
         w1_raw = load_rows("w1_raw", w1)
+        idx = load_list("idx", offs)
         for q in range(4):
             nc.sync.dma_start(tab_s[q:P:32, :].bitcast(I32), tab_scales[0, q:16:4, :].bitcast(I32))
         tab_w = sb.tile([P, T], I32, name="tab_w", tag="tab_w", align_bytes=64)
@@ -77,7 +78,7 @@ def tile_attend_ctriples_kernel(tc, tab_words, tab_scales, w1, bias, wo, dy, old
         s2 = sb.tile([P, J], F32, name="s2")
         s3 = sb.tile([P, J], F32, name="s3")
         for window in (s1, s2, s3):
-            nc.gpsimd.memset(window[:], 0.0)
+            nc.vector.memset(window[:], 0.0)
 
         ident = sb.tile([P, P], F32, name="ident")
         make_identity(nc, ident[:])
@@ -92,25 +93,29 @@ def tile_attend_ctriples_kernel(tc, tab_words, tab_scales, w1, bias, wo, dy, old
         w1_c, w1_s = quantise("w1", w1_bf[:])
         col_s = sb.tile([P, J], U8, name="col_s", tag="w1_bf", align_bytes=64)
         nc.vector.tensor_copy(col_s[:], tab_s[:].indirect(idx[:]))
-        a = []
-        for h, cols in enumerate(halves):
-            col_w = sb.tile([P, HALF], U32, name=f"col_w{h}", tag=("tab_s", "col_w1")[h], align_bytes=64)
+        col_w = []
+        for h in range(2):
+            words = sb.tile([P, HALF], U32, name=f"col_w{h}", tag=("tab_s", "col_w1")[h], align_bytes=64)
             nc.vector.tensor_copy(
-                col_w[:], tab_w[:].bitcast(U32).indirect(idx[:, h * HALF // 16 : (h + 1) * HALF // 16])
+                words[:], tab_w[:].bitcast(U32).indirect(idx[:, h * HALF // 16 : (h + 1) * HALF // 16])
             )
-            acc = psum.tile([P, HALF], F32, name=f"a{h}", tag=f"half{h}")
-            nc.tensor.matmul_mx(
-                out=acc[:], lhsT=w1_c[:].bitcast(FP8X4), lhsT_scale=w1_s[:],
-                rhs=col_w[:].bitcast(FP8X4), rhs_scale=col_s[:, cols], start=True, stop=True,
-            )
-            a.append(acc)
-
+            col_w.append(words)
+        spans = [slice(0, HALF), slice(HALF, HALF + P), slice(HALF + P, J)]
         sig_neg = sb.tile([P, J], F32, name="sig_neg")
         z = sb.tile([P, J], F32, name="z")
-        for h, cols in enumerate(halves):
-            nc.scalar.activation(sig_neg[:, cols], a[h][:], ACT.Sigmoid, bias=neg_b[:], scale=-1.0)
-        for h, cols in enumerate(halves):
-            nc.vector.tensor_scalar(z[:, cols], a[h][:], b[:], None, ALU.add)
+        a = []
+        for i, cols in enumerate(spans):
+            h = cols.start // HALF
+            acc = psum.tile([P, cols.stop - cols.start], F32, name=f"a{i}", tag=f"bank{i}")
+            nc.tensor.matmul_mx(
+                out=acc[:], lhsT=w1_c[:].bitcast(FP8X4), lhsT_scale=w1_s[:],
+                rhs=col_w[h][:, cols.start - h * HALF : cols.stop - h * HALF].bitcast(FP8X4),
+                rhs_scale=col_s[:, cols], start=True, stop=True,
+            )
+            nc.scalar.activation(sig_neg[:, cols], acc[:], ACT.Sigmoid, bias=neg_b[:], scale=-1.0)
+            a.append(acc)
+        for acc, cols in zip(a, spans):
+            nc.vector.tensor_scalar(z[:, cols], acc[:], b[:], None, ALU.add)
 
         back_bf = sb.tile([P, R + M, PACK], BF16, name="back_bf", tag="tab_w", align_bytes=64)
         interleave(back_bf[:, :R, :], wo_raw)
@@ -125,7 +130,7 @@ def tile_attend_ctriples_kernel(tc, tab_words, tab_scales, w1, bias, wo, dy, old
 
         ln_sig = sb.tile([P, J], F32, name="ln_sig")
         h1 = sb.tile([P, J], F32, name="h1")
-        for cols in halves:
+        for cols in blocks:
             nc.scalar.activation(ln_sig[:, cols], sig_neg[:, cols], ACT.Ln, bias=LN_FLOOR)
             nc.vector.scalar_tensor_tensor(h1[:, cols], ln_sig[:, cols], -1.0, z[:, cols], ALU.mult, ALU.max)
         warm_rs = sb.tile([P, 1], F32, name="warm_rs")
@@ -179,7 +184,6 @@ def tile_attend_ctriples_kernel(tc, tab_words, tab_scales, w1, bias, wo, dy, old
         sig = sb.tile([P, J], F32, name="sig", tag="late")
         nc.scalar.activation(sig[:], z[:], ACT.Sigmoid)
 
-        blocks = [slice(i * P, (i + 1) * P) for i in range(J // P)]
         turned = [psum.tile([P, P], F32, name=f"turned{i}") for i in range(len(blocks))]
         for i, cols in enumerate(blocks):
             nc.tensor.matmul(turned[i][:], s3[:, cols], ident[:], start=True, stop=False, is_transpose=True)
@@ -187,7 +191,7 @@ def tile_attend_ctriples_kernel(tc, tab_words, tab_scales, w1, bias, wo, dy, old
         for i, cols in enumerate(blocks):
             nc.tensor.matmul(turned[i][:], s1[:, cols], ident[:], start=False, stop=True, is_transpose=True)
             nc.scalar.copy(turned_sb[:, cols], turned[i][:])
-        s13 = [psum.tile([P, HALF], F32, name=f"s13_{h}", tag=f"half{h}") for h in range(2)]
+        s13 = [psum.tile([P, HALF], F32, name=f"s13_{h}", tag=f"bank{h}") for h in range(2)]
         for i, cols in enumerate(blocks):
             nc.tensor.transpose(s13[i // 2][:, blocks[i % 2]], turned_sb[:, cols], ident[:])
 
@@ -196,6 +200,8 @@ def tile_attend_ctriples_kernel(tc, tab_words, tab_scales, w1, bias, wo, dy, old
             nc.vector.tensor_tensor(y[h][:], s13[h][:], s2[:, cols], ALU.add)
         for h, cols in enumerate(halves):
             nc.vector.tensor_tensor(y[h][:], y[h][:], sig[:, cols], ALU.mult)
-        for h, cols in enumerate(halves):
-            nc.vector.tensor_tensor(y[h][:], y[h][:], old_sb[:, cols], ALU.add)
-            nc.sync.dma_start(out[:, cols], y[h][:])
+        for cols in spans:
+            h = cols.start // HALF
+            piece = y[h][:, cols.start - h * HALF : cols.stop - h * HALF]
+            nc.vector.tensor_tensor(piece, piece, old_sb[:, cols], ALU.add)
+            nc.sync.dma_start(out[:, cols], piece)

@@ -59,13 +59,13 @@ def tile_attend_ctriples_kernel(tc, tab_words, tab_scales, w1, bias, wo, dy, old
         tab_s = sb.tile([P, T], U8, name="tab_s", tag="tab_s", align_bytes=64)
         nc.vector.memset(tab_s[:].bitcast(I32), 0)
         w1_raw = load_rows("w1_raw", w1)
+        b = sb.tile([P, 1], F32, name="b")
+        nc.scalar.dma_start(b[:], bias)
         idx = load_list("idx", offs)
         for q in range(4):
             nc.sync.dma_start(tab_s[q:P:32, :].bitcast(I32), tab_scales[0, q:16:4, :].bitcast(I32))
         tab_w = sb.tile([P, T], I32, name="tab_w", tag="tab_w", align_bytes=64)
         nc.sync.dma_start(tab_w[:], tab_words[0].rearrange("p n t -> p (n t)").bitcast(I32))
-        b = sb.tile([P, 1], F32, name="b")
-        nc.sync.dma_start(b[:], bias)
         wo_raw = load_rows("wo_raw", wo)
         dy_raw = load_rows("dy_raw", dy)
         idx2 = load_list("idx2", offs2)
@@ -83,10 +83,8 @@ def tile_attend_ctriples_kernel(tc, tab_words, tab_scales, w1, bias, wo, dy, old
         ident = sb.tile([P, P], F32, name="ident")
         make_identity(nc, ident[:])
 
-        warm_sig = sb.tile([P, 1], F32, name="warm_sig")
-        nc.scalar.activation(warm_sig[:], s1[:, 0:1], ACT.Sigmoid)
         neg_b = sb.tile([P, 1], F32, name="neg_b")
-        nc.scalar.activation(neg_b[:], b[:], ACT.Copy, scale=-1.0)
+        nc.vector.tensor_scalar(neg_b[:], b[:], -1.0, None, ALU.mult)
 
         w1_bf = sb.tile([P, R, PACK], BF16, name="w1_bf", tag="w1_bf", align_bytes=64)
         interleave(w1_bf[:], w1_raw)
@@ -133,8 +131,6 @@ def tile_attend_ctriples_kernel(tc, tab_words, tab_scales, w1, bias, wo, dy, old
         for cols in blocks:
             nc.scalar.activation(ln_sig[:, cols], sig_neg[:, cols], ACT.Ln, bias=LN_FLOOR)
             nc.vector.scalar_tensor_tensor(h1[:, cols], ln_sig[:, cols], -1.0, z[:, cols], ALU.mult, ALU.max)
-        warm_rs = sb.tile([P, 1], F32, name="warm_rs")
-        nc.scalar.activation(warm_rs[:], ln_sig[:, J - 1 : J], ACT.Abs_reciprocal_sqrt, bias=1.0, scale=-1.0)
 
         g2 = sb.tile([P, M], F32, name="g2")
         g3 = sb.tile([P, M], F32, name="g3")
@@ -149,9 +145,6 @@ def tile_attend_ctriples_kernel(tc, tab_words, tab_scales, w1, bias, wo, dy, old
         root = sb.tile([P, M], F32, name="root", tag="late")
         inv = sb.tile([P, M], F32, name="inv")
 
-        def look_up(g, lst, i):
-            nc.vector.tensor_copy(g[:, parts[i]], h1[:].indirect(lst[:, lists[i]]))
-
         def times(product, x, y, i):
             nc.vector.tensor_tensor(product[:, parts[i]], x[:, parts[i]], y[:, parts[i]], ALU.mult)
 
@@ -163,19 +156,15 @@ def tile_attend_ctriples_kernel(tc, tab_words, tab_scales, w1, bias, wo, dy, old
             nc.vector.tensor_tensor(s3[:].indirect(idx4[:, lists[i]]), c23[:, parts[i]], inv[:, parts[i]], ALU.mult)
 
         nc.vector.tensor_copy(g2[:], h1[:].indirect(idx2[:]))
-        look_up(g3, idx3, 0)
-        look_up(g4, idx4, 0)
-        times(g23, g2, g3, 0)
-        look_up(g3, idx3, 1)
-        times(s, g23, g4, 0)
-        invert(0)
-        look_up(g4, idx4, 1)
-        times(g23, g2, g3, 1)
-        times(c23, c0, g23, 0)
-        times(s, g23, g4, 1)
-        invert(1)
+        nc.vector.tensor_copy(g3[:], h1[:].indirect(idx3[:]))
+        nc.vector.tensor_copy(g4[:], h1[:].indirect(idx4[:]))
+        for i in range(2):
+            times(g23, g2, g3, i)
+        for i in range(2):
+            times(s, g23, g4, i)
+            invert(i)
+        nc.vector.tensor_tensor(c23[:], c0[:], g23[:], ALU.mult)
         nc.vector.tensor_tensor(c4[:], c0[:], g4[:], ALU.mult)
-        times(c23, c0, g23, 1)
         place_e3(0)
         nc.vector.tensor_tensor(ds4[:], c4[:], inv[:], ALU.mult)
         place_e3(1)
@@ -200,8 +189,6 @@ def tile_attend_ctriples_kernel(tc, tab_words, tab_scales, w1, bias, wo, dy, old
             nc.vector.tensor_tensor(y[h][:], s13[h][:], s2[:, cols], ALU.add)
         for h, cols in enumerate(halves):
             nc.vector.tensor_tensor(y[h][:], y[h][:], sig[:, cols], ALU.mult)
-        for cols in spans:
-            h = cols.start // HALF
-            piece = y[h][:, cols.start - h * HALF : cols.stop - h * HALF]
-            nc.vector.tensor_tensor(piece, piece, old_sb[:, cols], ALU.add)
-            nc.sync.dma_start(out[:, cols], piece)
+        for h, cols in enumerate(halves):
+            nc.vector.tensor_tensor(y[h][:], y[h][:], old_sb[:, cols], ALU.add)
+            nc.sync.dma_start(out[:, cols], y[h][:])

from contextlib import ExitStack

import concourse.mybir as mybir
from concourse.masks import make_identity

K, R, F, T, J, M = 512, 128, 512, 2048, 512, 256
FLOPS = 2 * K * R * J + 2 * F * R * M

F32 = mybir.dt.float32
BF16 = mybir.dt.bfloat16
I32 = mybir.dt.int32
U32 = mybir.dt.uint32
U16 = mybir.dt.uint16
U8 = mybir.dt.uint8
FP8X4 = mybir.dt.float8_e4m3fn_x4
ALU = mybir.AluOpType
ACT = mybir.ActivationFunctionType

P = 128
PACK = 4
HALF = J // 2
LN_FLOOR = 2.0 ** -60


def tile_attend_ctriples_kernel(tc, tab_words, tab_scales, w1, bias, wo, dy, old, offs, offs2, offs3, offs4, out):
    nc = tc.nc
    halves = [slice(0, HALF), slice(HALF, J)]
    blocks = [slice(i * P, (i + 1) * P) for i in range(J // P)]

    with ExitStack() as ctx:
        sb = ctx.enter_context(tc.tile_pool(name="sb", bufs=1))
        psum = ctx.enter_context(tc.psum_pool(name="psum", bufs=1))

        def load_list(name, src):
            t = sb.tile(list(src.shape), U16, name=name)
            nc.sync.dma_start(t[:], src)
            return t

        def load_rows(name, src):
            t = sb.tile([P, PACK, src.shape[1]], F32, name=name)
            nc.sync.dma_start(t[:], src.rearrange("(p j) w -> p j w", j=PACK))
            return t

        def interleave(t, raw):
            nc.vector.tensor_copy(
                out=t.rearrange("p (c i) j -> p c j i", i=4),
                in_=raw[:].rearrange("p j (c i) -> p c j i", i=4),
            )

        def quantise(name, grouped):
            width = grouped.shape[1]
            codes = sb.tile([P, width], U32, name=name + "_codes", align_bytes=64)
            scales = sb.tile([P, width], U8, name=name + "_scales", align_bytes=64)
            nc.vector.quantize_mx(
                out=codes[:].bitcast(FP8X4), scales=scales[:], in_=grouped.rearrange("p w j -> p (w j)")
            )
            return codes, scales

        tab_s = sb.tile([P, T], U8, name="tab_s", tag="tab_s", align_bytes=64)
        nc.vector.memset(tab_s[:].bitcast(I32), 0)
        w1_raw = load_rows("w1_raw", w1)
        b = sb.tile([P, 1], F32, name="b")
        nc.scalar.dma_start(b[:], bias)
        idx = load_list("idx", offs)
        for q in range(4):
            nc.sync.dma_start(tab_s[q:P:32, :].bitcast(I32), tab_scales[0, q:16:4, :].bitcast(I32))
        tab_w = sb.tile([P, T], I32, name="tab_w", tag="tab_w", align_bytes=64)
        nc.sync.dma_start(tab_w[:], tab_words[0].rearrange("p n t -> p (n t)").bitcast(I32))
        wo_raw = load_rows("wo_raw", wo)
        dy_raw = load_rows("dy_raw", dy)
        idx2 = load_list("idx2", offs2)
        idx3 = load_list("idx3", offs3)
        idx4 = load_list("idx4", offs4)
        old_sb = sb.tile([P, J], F32, name="old_sb")
        nc.sync.dma_start(old_sb[:], old)

        s1 = sb.tile([P, J], F32, name="s1")
        s2 = sb.tile([P, J], F32, name="s2")
        s3 = sb.tile([P, J], F32, name="s3")
        for window in (s1, s2, s3):
            nc.vector.memset(window[:], 0.0)

        ident = sb.tile([P, P], F32, name="ident")
        make_identity(nc, ident[:])

        neg_b = sb.tile([P, 1], F32, name="neg_b")
        nc.vector.tensor_scalar(neg_b[:], b[:], -1.0, None, ALU.mult)

        w1_bf = sb.tile([P, R, PACK], BF16, name="w1_bf", tag="w1_bf", align_bytes=64)
        interleave(w1_bf[:], w1_raw)
        w1_c, w1_s = quantise("w1", w1_bf[:])
        col_s = sb.tile([P, J], U8, name="col_s", tag="w1_bf", align_bytes=64)
        nc.vector.tensor_copy(col_s[:], tab_s[:].indirect(idx[:]))
        col_w = []
        for h in range(2):
            words = sb.tile([P, HALF], U32, name=f"col_w{h}", tag=("tab_s", "col_w1")[h], align_bytes=64)
            nc.vector.tensor_copy(
                words[:], tab_w[:].bitcast(U32).indirect(idx[:, h * HALF // 16 : (h + 1) * HALF // 16])
            )
            col_w.append(words)
        spans = [slice(0, HALF), slice(HALF, HALF + P), slice(HALF + P, J)]
        sig_neg = sb.tile([P, J], F32, name="sig_neg")
        z = sb.tile([P, J], F32, name="z")
        a = []
        for i, cols in enumerate(spans):
            h = cols.start // HALF
            acc = psum.tile([P, cols.stop - cols.start], F32, name=f"a{i}", tag=f"bank{i}")
            nc.tensor.matmul_mx(
                out=acc[:], lhsT=w1_c[:].bitcast(FP8X4), lhsT_scale=w1_s[:],
                rhs=col_w[h][:, cols.start - h * HALF : cols.stop - h * HALF].bitcast(FP8X4),
                rhs_scale=col_s[:, cols], start=True, stop=True,
            )
            nc.scalar.activation(sig_neg[:, cols], acc[:], ACT.Sigmoid, bias=neg_b[:], scale=-1.0)
            a.append(acc)
        for acc, cols in zip(a, spans):
            nc.vector.tensor_scalar(z[:, cols], acc[:], b[:], None, ALU.add)

        back_bf = sb.tile([P, R + M, PACK], BF16, name="back_bf", tag="tab_w", align_bytes=64)
        interleave(back_bf[:, :R, :], wo_raw)
        interleave(back_bf[:, R:, :], dy_raw)
        wo_c, wo_s = quantise("wo", back_bf[:, :R, :])
        dy_c, dy_s = quantise("dy", back_bf[:, R:, :])
        c0 = psum.tile([P, M], F32, name="c0")
        nc.tensor.matmul_mx(
            out=c0[:], lhsT=wo_c[:].bitcast(FP8X4), lhsT_scale=wo_s[:],
            rhs=dy_c[:].bitcast(FP8X4), rhs_scale=dy_s[:], start=True, stop=True,
        )

        ln_sig = sb.tile([P, J], F32, name="ln_sig")
        h1 = sb.tile([P, J], F32, name="h1")
        for cols in blocks:
            nc.scalar.activation(ln_sig[:, cols], sig_neg[:, cols], ACT.Ln, bias=LN_FLOOR)
            nc.vector.scalar_tensor_tensor(h1[:, cols], ln_sig[:, cols], -1.0, z[:, cols], ALU.mult, ALU.max)

        g2 = sb.tile([P, M], F32, name="g2")
        g3 = sb.tile([P, M], F32, name="g3")
        g4 = sb.tile([P, M], F32, name="g4")
        g23 = sb.tile([P, M], F32, name="g23")
        s = sb.tile([P, M], F32, name="s")
        parts = [slice(0, M // 2), slice(M // 2, M)]
        lists = [slice(0, M // 32), slice(M // 32, M // 16)]
        c23 = sb.tile([P, M], F32, name="c23")
        c4 = sb.tile([P, M], F32, name="c4")
        ds4 = sb.tile([P, M], F32, name="ds4")
        root = sb.tile([P, M], F32, name="root", tag="late")
        inv = sb.tile([P, M], F32, name="inv")

        def times(product, x, y, i):
            nc.vector.tensor_tensor(product[:, parts[i]], x[:, parts[i]], y[:, parts[i]], ALU.mult)

        def invert(i):
            nc.scalar.activation(root[:, parts[i]], s[:, parts[i]], ACT.Abs_reciprocal_sqrt, bias=1.0)
            nc.scalar.activation(inv[:, parts[i]], root[:, parts[i]], ACT.Square)

        def place_e3(i):
            nc.vector.tensor_tensor(s3[:].indirect(idx4[:, lists[i]]), c23[:, parts[i]], inv[:, parts[i]], ALU.mult)

        nc.vector.tensor_copy(g2[:], h1[:].indirect(idx2[:]))
        nc.vector.tensor_copy(g3[:], h1[:].indirect(idx3[:]))
        nc.vector.tensor_copy(g4[:], h1[:].indirect(idx4[:]))
        for i in range(2):
            times(g23, g2, g3, i)
        for i in range(2):
            times(s, g23, g4, i)
            invert(i)
        nc.vector.tensor_tensor(c23[:], c0[:], g23[:], ALU.mult)
        nc.vector.tensor_tensor(c4[:], c0[:], g4[:], ALU.mult)
        place_e3(0)
        nc.vector.tensor_tensor(ds4[:], c4[:], inv[:], ALU.mult)
        place_e3(1)
        nc.vector.tensor_tensor(s1[:].indirect(idx2[:]), ds4[:], g3[:], ALU.mult)
        nc.vector.tensor_tensor(s2[:].indirect(idx3[:]), ds4[:], g2[:], ALU.mult)
        sig = sb.tile([P, J], F32, name="sig", tag="late")
        nc.scalar.activation(sig[:], z[:], ACT.Sigmoid)

        turned = [psum.tile([P, P], F32, name=f"turned{i}") for i in range(len(blocks))]
        for i, cols in enumerate(blocks):
            nc.tensor.matmul(turned[i][:], s3[:, cols], ident[:], start=True, stop=False, is_transpose=True)
        turned_sb = sb.tile([P, J], F32, name="turned_sb")
        for i, cols in enumerate(blocks):
            nc.tensor.matmul(turned[i][:], s1[:, cols], ident[:], start=False, stop=True, is_transpose=True)
            nc.scalar.copy(turned_sb[:, cols], turned[i][:])
        s13 = [psum.tile([P, HALF], F32, name=f"s13_{h}", tag=f"bank{h}") for h in range(2)]
        for i, cols in enumerate(blocks):
            nc.tensor.transpose(s13[i // 2][:, blocks[i % 2]], turned_sb[:, cols], ident[:])

        y = [sb.tile([P, HALF], F32, name=f"y{h}") for h in range(2)]
        for h, cols in enumerate(halves):
            nc.vector.tensor_tensor(y[h][:], s13[h][:], s2[:, cols], ALU.add)
        for h, cols in enumerate(halves):
            nc.vector.tensor_tensor(y[h][:], y[h][:], sig[:, cols], ALU.mult)
        for h, cols in enumerate(halves):
            nc.vector.tensor_tensor(y[h][:], y[h][:], old_sb[:, cols], ALU.add)
            nc.sync.dma_start(out[:, cols], y[h][:])
